import numpy as np
import ml_dtypes


def mxq(x, axis, fmt="e4m3"):
    dtype, down = {"e4m3": (ml_dtypes.float8_e4m3fn, 7), "e5m2": (ml_dtypes.float8_e5m2, 14)}[fmt]
    v = np.moveaxis(np.asarray(x, np.float32).astype(ml_dtypes.bfloat16).astype(np.float64), axis, -1)
    blocks = v.reshape(v.shape[:-1] + (-1, 32))
    amax = np.abs(blocks).max(-1, keepdims=True)
    byte = np.maximum(np.where(amax > 0, np.frexp(amax)[1] - 1 + 127, 0) - down, 1)
    scale = np.exp2(byte - 127.0)
    codes = (blocks / scale).astype(np.float32).astype(dtype).astype(np.float64)
    return np.moveaxis((codes * scale).reshape(v.shape), -1, axis)


WIDE = False


def mx_kscale(k):
    if not WIDE:
        return np.ones(k)
    levels = np.array([10, -10, 5, -5, 0])
    if k % 512:
        return np.exp2(np.random.permutation(np.resize(levels, k // 32))).repeat(32)
    a = np.empty((k // 512, 16))
    for p in range(k // 512):
        a[p, :8] = np.random.permutation(np.resize(levels, 8))
        for g in range(8):
            far = levels[np.abs(levels - a[p, g]) >= 10]
            a[p, g + 8] = far[np.random.randint(len(far))]
    return np.exp2(a.ravel()).repeat(32)


def f64(x):
    return np.asarray(x).astype(np.float64)


def striped(idx):
    return np.tile(idx.reshape(-1, 16).T, (8, 1)).astype(np.uint16)


def unstriped(offs):
    return offs[:16].T.reshape(-1).astype(np.int64)


def pack_weight(w):
    k, n = w.shape
    w = f64(np.asarray(w, np.float32).astype(ml_dtypes.bfloat16)).reshape(k // 32, 32, n)
    amax = np.abs(w).max(1)
    byte = np.clip(np.where(amax > 0, np.frexp(amax)[1] - 1 + 127 - 7, 1), 1, 254)
    scaled = (w * np.exp2(127.0 - byte)[:, None, :]).reshape(k, n).astype(np.float32)
    words = np.ascontiguousarray(scaled.reshape(k // 512, 128, 4, n).transpose(0, 1, 3, 2)).astype(ml_dtypes.float8_e4m3fn).view(np.uint8)
    return words, np.ascontiguousarray(byte.astype(np.uint8).reshape(k // 512, 16, n))


def unpack_weight(words, scales):
    g, p, n, _ = words.shape
    vals = np.ascontiguousarray(words).view(ml_dtypes.float8_e4m3fn).astype(np.float64) * np.repeat(np.exp2(scales.astype(np.float64) - 127.0), 8, axis=1)[..., None]
    return vals.transpose(0, 1, 3, 2).reshape(g * 512, n)


def silu(v):
    return v / (1.0 + np.exp(-np.maximum(v, -700.0)))


K, T, H, N, J, U = 1024, 1024, 512, 128, 512, 2048


def setup_inputs():
    n = np.random.standard_normal
    s = mx_kscale(K)[:, None]
    u = mx_kscale(H)
    r = mx_kscale(J)[:, None]
    packed_xT = pack_weight(n((K, T)) * s)
    return {
        "x_words": packed_xT[0],
        "x_scales": packed_xT[1],
        "aT": (n((J, U)) * r).astype(np.float32),
        "w1": (n((K, H)) / np.sqrt(K) / s * u).astype(np.float32),
        "w3": (n((J, H)) / np.sqrt(J) / r).astype(np.float32),
        "w2": (n((H, N)) / np.sqrt(2 * H) / u[:, None]).astype(np.float32),
        "pos1": striped(np.random.permutation(T)),
        "pos2": striped(np.random.permutation(T)),
    }


def reference(x_words, x_scales, aT, w1, w3, w2, pos1, pos2):
    xq = unpack_weight(x_words, x_scales)
    h = silu(mxq(f64(w1), 0, "e4m3").T @ xq)
    f = mxq(f64(w3), 0, "e4m3").T @ mxq(f64(aT), 0, "e4m3")
    z = h[:, unstriped(pos1)] * f[:, :T] + h[:, unstriped(pos2)] * f[:, T:2 * T]
    return mxq(f64(w2), 0, "e4m3").T @ mxq(z, 0, "e4m3")

@@ -1,0 +1,256 @@
+from contextlib import ExitStack
+
+import concourse.mybir as mybir
+from concourse.masks import make_identity
+
+K, T, H, N, J, D = 1024, 1024, 512, 128, 512, 2
+FLOPS = 2 * (K * H * T + J * H * D * T + H * N * T)
+
+F32 = mybir.dt.float32
+BF16 = mybir.dt.bfloat16
+I32 = mybir.dt.int32
+U32 = mybir.dt.uint32
+U16 = mybir.dt.uint16
+U8 = mybir.dt.uint8
+FP8X4 = mybir.dt.float8_e4m3fn_x4
+SILU = mybir.ActivationFunctionType.Silu
+MULT = mybir.AluOpType.mult
+
+P = 128
+PACK = 4
+BANK = 512
+TILES = H // P
+PASSES = K // (P * PACK)
+HALF = T // 2
+LOAD = 256
+CHUNKS = ((0, 256), (256, 256), (512, 256), (768, 128), (896, 128))
+
+
+def interleave(copy, staged, raw):
+    copy(
+        out=staged.rearrange("p (c i j) -> p c j i", i=4, j=PACK),
+        in_=raw.rearrange("p j (c i) -> p c j i", i=4),
+    )
+
+
+def tile_picked_wdime_none_l_kernel(
+    tc, x_words, x_scales, aT, w1, w3, w2, pos1, pos2, out
+):
+    nc = tc.nc
+    with ExitStack() as ctx:
+        keep = ctx.enter_context(tc.tile_pool(name="keep", bufs=1))
+        ring = ctx.enter_context(tc.tile_pool(name="ring", bufs=2))
+        psum = ctx.enter_context(tc.psum_pool(name="psum", bufs=1))
+
+        def held(name, width, dtype):
+            return keep.tile([P, width], dtype, name=name, align_bytes=64)
+
+        def quantize(name, staged):
+            words = staged.shape[1] // PACK
+            codes = held(name + "_codes", words, U32)
+            scales = held(name + "_scales", words, U8)
+            nc.vector.quantize_mx(out=codes[:].bitcast(FP8X4), scales=scales[:], in_=staged)
+            return codes, scales
+
+        def product(acc, lhs, lhs_cols, rhs_codes, rhs_scales, start=True, stop=True):
+            nc.tensor.matmul_mx(
+                out=acc,
+                lhsT=lhs[0][:, lhs_cols].bitcast(FP8X4),
+                lhsT_scale=lhs[1][:, lhs_cols],
+                rhs=rhs_codes.bitcast(FP8X4),
+                rhs_scale=rhs_scales,
+                start=start,
+                stop=stop,
+            )
+
+        x_planes = held("x_planes", T, U8)
+        nc.vector.memset(x_planes[:].bitcast(U32), 0)
+
+        w1_rows = w1.rearrange("(z p j) c -> z p j c", z=PASSES, j=PACK)
+
+        def load_w1(name, c0, c1):
+            tiles = []
+            for z in range(PASSES):
+                raw = keep.tile([P, PACK, c1 - c0], F32, name="%s_%d" % (name, z))
+                nc.sync.dma_start(out=raw[:], in_=w1_rows[z][:, :, c0:c1])
+                tiles.append(raw)
+            return tiles
+
+        w1_raw0 = load_w1("w1_raw0", 0, P)
+        for q in range(4):
+            nc.sync.dma_start(
+                out=x_planes[32 * q : 32 * q + 4 * PASSES, :].bitcast(I32),
+                in_=x_scales[:, 4 * q : 4 * q + 4, :].bitcast(I32),
+            )
+        x_rows = x_words.rearrange("z p c r -> p z (c r)")
+        x_codes = []
+        for half in range(2):
+            codes = keep.tile([P, PASSES, HALF], U32, name="x_codes%d" % half, align_bytes=64)
+            nc.sync.dma_start(
+                out=codes[:].bitcast(I32),
+                in_=x_rows[:, :, PACK * HALF * half : PACK * HALF * (half + 1)].bitcast(I32),
+            )
+            x_codes.append(codes)
+        w1_raw1 = load_w1("w1_raw1", P, 2 * P)
+        lists = []
+        for d, pos in enumerate((pos1, pos2)):
+            offsets = keep.tile([P, T // 16], U16, name="pos%d" % d)
+            nc.sync.dma_start(offsets[:], pos)
+            lists.append(offsets)
+        w3_raw = keep.tile([P, PACK, H], F32, name="w3_raw")
+        nc.sync.dma_start(out=w3_raw[:], in_=w3.rearrange("(p j) c -> p j c", j=PACK))
+        w1_raw23 = load_w1("w1_raw23", 2 * P, 4 * P)
+        a_rows = aT.rearrange("(p j) (d v) -> p (j d) v", j=PACK, d=D)
+        a_raw = []
+        w2_raw = keep.tile([P, PACK, N], F32, name="w2_raw")
+        for c in range(T // LOAD):
+            raw = keep.tile([P, PACK * D, LOAD], F32, name="a_raw%d" % c)
+            nc.sync.dma_start(out=raw[:], in_=a_rows[:, :, LOAD * c : LOAD * (c + 1)])
+            a_raw.append(raw)
+            if c == 1:
+                nc.sync.dma_start(out=w2_raw[:], in_=w2.rearrange("(p j) m -> p j m", j=PACK))
+
+        identity = keep.tile([P, P], F32, name="identity")
+        make_identity(nc, identity[:])
+
+        early = {(t, half): held("early%d%d" % (t, half), (D + 1) * HALF, F32) for t in range(2) for half in range(2)}
+
+        def early_view(t, half):
+            return early[t, half][:, HALF:].rearrange("p (d v) -> p d v", d=D)
+
+        h = []
+
+        def h_tile(t, copy, staged, raws):
+            for z in range(PASSES):
+                interleave(copy, staged[:, BANK * z : BANK * (z + 1)], raws[z])
+            w1_q = quantize("w1_%d" % t, staged)
+            h_t = keep.tile([P, T], F32, name="h%d" % t)
+            for half in range(2):
+                acc = psum.tile([P, BANK], F32, name="acc", bufs=4)
+                for z in range(PASSES):
+                    product(
+                        acc[:], w1_q, slice(P * z, P * (z + 1)),
+                        x_codes[half][:, z, :], x_planes[4 * z :, HALF * half : HALF * (half + 1)],
+                        start=(z == 0), stop=(z == PASSES - 1),
+                    )
+                nc.scalar.activation(out=h_t[:, HALF * half : HALF * (half + 1)], in_=acc[:], func=SILU)
+            h.append(h_t)
+
+        def gather(t, v0, width, into):
+            for d in range(D):
+                offsets = lists[d][:, v0 // 16 : (v0 + width) // 16]
+                nc.vector.tensor_copy(out=into[:, d, :], in_=h[t][:].indirect(offsets))
+
+        def gather_early(t, half):
+            gather(t, HALF * half, HALF, early_view(t, half))
+
+        def quantize_a(c, staged):
+            interleave(nc.scalar.copy, staged, a_raw[c][:].rearrange("p (j d) v -> p j (d v)", j=PACK))
+            return quantize("a%d" % c, staged)
+
+        def a_ring():
+            return ring.tile([P, PACK * D * LOAD], BF16, name="a_staged", align_bytes=64)[:]
+
+        h_tile(0, nc.vector.tensor_copy, held("w1_staged0", 2 * BANK, BF16)[:], [r[:] for r in w1_raw0])
+        h_tile(1, nc.vector.tensor_copy, held("w1_staged1", 2 * BANK, BF16)[:], [r[:] for r in w1_raw1])
+        gather_early(0, 0)
+        gather_early(0, 1)
+        staged = held("w3_staged", PACK * H, BF16)[:]
+        for t in range(TILES):
+            interleave(nc.scalar.copy, staged[:, BANK * t : BANK * (t + 1)], w3_raw[:, :, P * t : P * (t + 1)])
+        w3_q = quantize("w3", staged)
+        h_tile(2, nc.scalar.copy, early[1, 0][:, 2 * HALF :].bitcast(BF16), [r[:, :, :P] for r in w1_raw23])
+        a_q = [quantize_a(0, early[1, 1][:, : 2 * HALF].bitcast(BF16))]
+        h_tile(3, nc.scalar.copy, early[1, 1][:, 2 * HALF :].bitcast(BF16), [r[:, :, P:] for r in w1_raw23])
+        gather_early(1, 0)
+        gather_early(1, 1)
+
+        steps = [(v0, width, t) for v0, width in CHUNKS for t in range(TILES)]
+        filters, z_rows, z_sums = {}, {}, {}
+
+        def filter_product(n):
+            v0, width, t = steps[n]
+            load, in_load = divmod(v0, LOAD)
+            a_codes, a_scales = a_q[load]
+            share = BANK // (D * width)
+            if t % share == 0:
+                bank = psum.tile([P, share, D, width], F32, name="acc", bufs=4)
+                for tt in range(share):
+                    filters[n + tt] = bank[:, tt, :, :]
+                    for d in range(D):
+                        cols = slice(LOAD * d + in_load, LOAD * d + in_load + width)
+                        product(bank[:, tt, d, :], w3_q, slice(P * (t + tt), P * (t + tt + 1)), a_codes[:, cols], a_scales[:, cols])
+
+        def multiply(n):
+            v0, width, t = steps[n]
+            blocks = width // P
+            half, in_half = divmod(v0, HALF)
+            pair, tt = divmod(t, 2)
+            picked = early_view(tt, half)[:, :, in_half : in_half + width]
+            terms = ring.tile([P, D, width], F32, name="terms", bufs=4)
+            nc.vector.tensor_tensor(
+                out=terms[:], in0=filters[n], in1=picked, op=MULT
+            )
+            if pair == 0:
+                gather(t + 2, v0, width, picked)
+            if t == 0:
+                z_rows[v0] = ring.tile([P, blocks * H], BF16, name="z_rows")
+            if tt == 0:
+                z_sums[v0, pair] = psum.tile([P, blocks, 2 * P], F32, name="z_sum", bufs=2)
+            z_sum = z_sums[v0, pair]
+            for b in range(blocks):
+                for d in range(D):
+                    nc.tensor.matmul(
+                        z_sum[:, b, P * tt : P * (tt + 1)],
+                        lhsT=terms[:, d, P * b : P * (b + 1)],
+                        rhs=identity[:],
+                        is_transpose=True,
+                        start=(d == 0),
+                        stop=(d == D - 1),
+                    )
+            if tt == 1:
+                z_view = z_rows[v0][:].rearrange("v (b u p e) -> v b u p e", b=blocks, u=2, e=2)
+                nc.scalar.copy(
+                    out=z_view[:, :, :, 64 * pair : 64 * (pair + 1), :],
+                    in_=z_sum[:].rearrange("v b (p u e) -> v b u p e", u=2, e=2),
+                )
+
+        def project(v0, width):
+            blocks = width // P
+            words = z_rows[v0][:].bitcast(F32)
+            back = psum.tile([P, blocks, 2, P], F32, name="back", bufs=1)
+            for b in range(blocks):
+                for u in range(2):
+                    nc.tensor.transpose(back[:, b, u, :], words[:, P * (2 * b + u) : P * (2 * b + u + 1)], identity[:])
+            z_staged = ring.tile([P, PACK * width], BF16, name="z_staged", align_bytes=64)
+            nc.scalar.copy(
+                out=z_staged[:].bitcast(F32).rearrange("p (b v u) -> p b v u", b=blocks, u=2),
+                in_=back[:].rearrange("p b u v -> p b v u"),
+            )
+            z_codes, z_scales = quantize("z%d" % v0, z_staged[:])
+            result = psum.tile([P, width], F32, name="result")
+            product(result[:], w2_q, slice(0, N), z_codes[:], z_scales[:])
+            stored = ring.tile([P, width], F32, name="stored")
+            nc.scalar.copy(out=stored[:], in_=result[:])
+            nc.sync.dma_start(out=out[:, v0 : v0 + width], in_=stored[:])
+
+        LEAD, TAIL = 2, 1
+        for n in range(LEAD):
+            filter_product(n)
+        for n in range(len(steps) + TAIL):
+            if n == 0:
+                a_q.append(quantize_a(1, a_ring()))
+            if n == 2:
+                staged = held("w2_staged", PACK * N, BF16)[:]
+                interleave(nc.scalar.copy, staged, w2_raw[:])
+                w2_q = quantize("w2", staged)
+            if n == 4:
+                a_q.append(quantize_a(2, a_ring()))
+            if n == 8:
+                a_q.append(quantize_a(3, a_ring()))
+            if n + LEAD < len(steps):
+                filter_product(n + LEAD)
+            if n < len(steps):
+                multiply(n)
+            if n >= TAIL and steps[n - TAIL][2] == TILES - 1:
+                project(*steps[n - TAIL][:2])

@@ -1,7 +1,6 @@
 from contextlib import ExitStack
 
 import concourse.mybir as mybir
-from concourse.masks import make_identity
 
 K, T, H, N, J, D = 1024, 1024, 512, 128, 512, 2
 FLOPS = 2 * (K * H * T + J * H * D * T + H * N * T)
@@ -15,6 +14,7 @@ U8 = mybir.dt.uint8
 FP8X4 = mybir.dt.float8_e4m3fn_x4
 SILU = mybir.ActivationFunctionType.Silu
 MULT = mybir.AluOpType.mult
+ADD = mybir.AluOpType.add
 
 P = 128
 PACK = 4
@@ -23,13 +23,23 @@ TILES = H // P
 PASSES = K // (P * PACK)
 HALF = T // 2
 LOAD = 256
-CHUNKS = ((0, 256), (256, 256), (512, 256), (768, 128), (896, 128))
+CHUNKS = T // LOAD
+X_PIECES = ((0, 512), (512, 512))
+PLAIN = (2, 2, 2, 2)
+RUN = 2
 
 
 def interleave(copy, staged, raw):
     copy(
-        out=staged.rearrange("p (c i j) -> p c j i", i=4, j=PACK),
-        in_=raw.rearrange("p j (c i) -> p c j i", i=4),
+        out=staged.rearrange("p (c i j) -> p c j i", i=RUN, j=PACK),
+        in_=raw.rearrange("p j (c i) -> p c j i", i=RUN),
+    )
+
+
+def deal(copy, staged, raw, t):
+    copy(
+        out=staged.rearrange("p (b r i j) -> p b r j i", b=16, i=RUN, j=PACK),
+        in_=raw.rearrange("p j (b t r i) -> p t b r j i", b=16, t=TILES, i=RUN)[:, t],
     )
 
 
@@ -66,17 +76,11 @@ def tile_picked_wdime_none_l_kernel(
         x_planes = held("x_planes", T, U8)
         nc.vector.memset(x_planes[:].bitcast(U32), 0)
 
-        w1_rows = w1.rearrange("(z p j) c -> z p j c", z=PASSES, j=PACK)
-
-        def load_w1(name, c0, c1):
-            tiles = []
-            for z in range(PASSES):
-                raw = keep.tile([P, PACK, c1 - c0], F32, name="%s_%d" % (name, z))
-                nc.sync.dma_start(out=raw[:], in_=w1_rows[z][:, :, c0:c1])
-                tiles.append(raw)
-            return tiles
-
-        w1_raw0 = load_w1("w1_raw0", 0, P)
+        w1_raw = []
+        for z in range(PASSES):
+            raw = keep.tile([P, PACK, H], F32, name="w1_raw%d" % z)
+            nc.sync.dma_start(out=raw[:], in_=w1.rearrange("(z p j) c -> z p j c", z=PASSES, j=PACK)[z])
+            w1_raw.append(raw)
         for q in range(4):
             nc.sync.dma_start(
                 out=x_planes[32 * q : 32 * q + 4 * PASSES, :].bitcast(I32),
@@ -84,14 +88,13 @@ def tile_picked_wdime_none_l_kernel(
             )
         x_rows = x_words.rearrange("z p c r -> p z (c r)")
         x_codes = []
-        for half in range(2):
-            codes = keep.tile([P, PASSES, HALF], U32, name="x_codes%d" % half, align_bytes=64)
+        for c0, width in X_PIECES:
+            codes = keep.tile([P, PASSES, width], U32, name="x_codes%d" % c0, align_bytes=64)
             nc.sync.dma_start(
                 out=codes[:].bitcast(I32),
-                in_=x_rows[:, :, PACK * HALF * half : PACK * HALF * (half + 1)].bitcast(I32),
+                in_=x_rows[:, :, PACK * c0 : PACK * (c0 + width)].bitcast(I32),
             )
             x_codes.append(codes)
-        w1_raw1 = load_w1("w1_raw1", P, 2 * P)
         lists = []
         for d, pos in enumerate((pos1, pos2)):
             offsets = keep.tile([P, T // 16], U16, name="pos%d" % d)
@@ -99,7 +102,6 @@ def tile_picked_wdime_none_l_kernel(
             lists.append(offsets)
         w3_raw = keep.tile([P, PACK, H], F32, name="w3_raw")
         nc.sync.dma_start(out=w3_raw[:], in_=w3.rearrange("(p j) c -> p j c", j=PACK))
-        w1_raw23 = load_w1("w1_raw23", 2 * P, 4 * P)
         a_rows = aT.rearrange("(p j) (d v) -> p (j d) v", j=PACK, d=D)
         a_raw = []
         w2_raw = keep.tile([P, PACK, N], F32, name="w2_raw")
@@ -108,41 +110,43 @@ def tile_picked_wdime_none_l_kernel(
             nc.sync.dma_start(out=raw[:], in_=a_rows[:, :, LOAD * c : LOAD * (c + 1)])
             a_raw.append(raw)
             if c == 1:
-                nc.sync.dma_start(out=w2_raw[:], in_=w2.rearrange("(p j) m -> p j m", j=PACK))
+                for t in range(TILES):
+                    nc.sync.dma_start(out=w2_raw[:, t, :], in_=w2.rearrange("(b t r) m -> t b r m", t=TILES, r=8)[t])
 
-        identity = keep.tile([P, P], F32, name="identity")
-        make_identity(nc, identity[:])
-
-        early = {(t, half): held("early%d%d" % (t, half), (D + 1) * HALF, F32) for t in range(2) for half in range(2)}
-
-        def early_view(t, half):
-            return early[t, half][:, HALF:].rearrange("p (d v) -> p d v", d=D)
+        w1_q = {}
+        for z in range(PASSES):
+            staged = [held("w1_staged%d%d" % (z, t), BANK, BF16)[:] for t in range(TILES)]
+            deal(nc.vector.tensor_copy, staged[0], w1_raw[z][:], 0)
+            for t in range(TILES):
+                if t + 1 < TILES:
+                    deal(nc.vector.tensor_copy, staged[t + 1], w1_raw[z][:], t + 1)
+                w1_q[z, t] = quantize("w1_%d%d" % (z, t), staged[t])
 
         h = []
 
-        def h_tile(t, copy, staged, raws):
-            for z in range(PASSES):
-                interleave(copy, staged[:, BANK * z : BANK * (z + 1)], raws[z])
-            w1_q = quantize("w1_%d" % t, staged)
+        def h_tile(t):
             h_t = keep.tile([P, T], F32, name="h%d" % t)
-            for half in range(2):
-                acc = psum.tile([P, BANK], F32, name="acc", bufs=4)
+            for codes, (c0, width) in zip(x_codes, X_PIECES):
+                acc = psum.tile([P, width], F32, name="acc", bufs=6)
                 for z in range(PASSES):
                     product(
-                        acc[:], w1_q, slice(P * z, P * (z + 1)),
-                        x_codes[half][:, z, :], x_planes[4 * z :, HALF * half : HALF * (half + 1)],
+                        acc[:], w1_q[z, t], slice(0, P),
+                        codes[:, z, :], x_planes[4 * z :, c0 : c0 + width],
                         start=(z == 0), stop=(z == PASSES - 1),
                     )
-                nc.scalar.activation(out=h_t[:, HALF * half : HALF * (half + 1)], in_=acc[:], func=SILU)
+                nc.scalar.activation(out=h_t[:, c0 : c0 + width], in_=acc[:], func=SILU)
             h.append(h_t)
 
-        def gather(t, v0, width, into):
-            for d in range(D):
-                offsets = lists[d][:, v0 // 16 : (v0 + width) // 16]
-                nc.vector.tensor_copy(out=into[:, d, :], in_=h[t][:].indirect(offsets))
+        early = {}
+
+        def early_tile(t, half):
+            early[t, half] = held("early%d%d" % (t, half), D * HALF, F32)
+            return early[t, half]
 
         def gather_early(t, half):
-            gather(t, HALF * half, HALF, early_view(t, half))
+            for d in range(D):
+                offsets = lists[d][:, HALF // 16 * half : HALF // 16 * (half + 1)]
+                nc.vector.tensor_copy(out=early[t, half][:, HALF * d : HALF * (d + 1)], in_=h[t][:].indirect(offsets))
 
         def quantize_a(c, staged):
             interleave(nc.scalar.copy, staged, a_raw[c][:].rearrange("p (j d) v -> p j (d v)", j=PACK))
@@ -151,93 +155,79 @@ def tile_picked_wdime_none_l_kernel(
         def a_ring():
             return ring.tile([P, PACK * D * LOAD], BF16, name="a_staged", align_bytes=64)[:]
 
-        h_tile(0, nc.vector.tensor_copy, held("w1_staged0", 2 * BANK, BF16)[:], [r[:] for r in w1_raw0])
-        h_tile(1, nc.vector.tensor_copy, held("w1_staged1", 2 * BANK, BF16)[:], [r[:] for r in w1_raw1])
-        gather_early(0, 0)
-        gather_early(0, 1)
-        staged = held("w3_staged", PACK * H, BF16)[:]
+        units = [(t, half) for t in range(TILES) for half in range(2) if t < PLAIN[2 * half]]
+        for unit in units:
+            early_tile(*unit)
+        h_tile(0)
+        h_tile(1)
+        for unit in units[:-2]:
+            gather_early(*unit)
+        staged = early[units[-2]][:].bitcast(BF16)
         for t in range(TILES):
-            interleave(nc.scalar.copy, staged[:, BANK * t : BANK * (t + 1)], w3_raw[:, :, P * t : P * (t + 1)])
+            deal(nc.scalar.copy, staged[:, BANK * t : BANK * (t + 1)], w3_raw[:], t)
         w3_q = quantize("w3", staged)
-        h_tile(2, nc.scalar.copy, early[1, 0][:, 2 * HALF :].bitcast(BF16), [r[:, :, :P] for r in w1_raw23])
-        a_q = [quantize_a(0, early[1, 1][:, : 2 * HALF].bitcast(BF16))]
-        h_tile(3, nc.scalar.copy, early[1, 1][:, 2 * HALF :].bitcast(BF16), [r[:, :, P:] for r in w1_raw23])
-        gather_early(1, 0)
-        gather_early(1, 1)
+        gather_early(*units[-2])
+        a_q = [quantize_a(0, early[units[-1]][:].bitcast(BF16))]
+        gather_early(*units[-1])
+        h_tile(2)
+        h_tile(3)
 
-        steps = [(v0, width, t) for v0, width in CHUNKS for t in range(TILES)]
-        filters, z_rows, z_sums = {}, {}, {}
+        steps = [(c, t) for c in range(CHUNKS) for t in range(TILES)]
+        filters, terms = {}, {}
 
         def filter_product(n):
-            v0, width, t = steps[n]
-            load, in_load = divmod(v0, LOAD)
-            a_codes, a_scales = a_q[load]
-            share = BANK // (D * width)
-            if t % share == 0:
-                bank = psum.tile([P, share, D, width], F32, name="acc", bufs=4)
-                for tt in range(share):
-                    filters[n + tt] = bank[:, tt, :, :]
-                    for d in range(D):
-                        cols = slice(LOAD * d + in_load, LOAD * d + in_load + width)
-                        product(bank[:, tt, d, :], w3_q, slice(P * (t + tt), P * (t + tt + 1)), a_codes[:, cols], a_scales[:, cols])
+            c, t = steps[n]
+            a_codes, a_scales = a_q[c]
+            bank = psum.tile([P, BANK], F32, name="acc", bufs=6)
+            product(bank[:], w3_q, slice(P * t, P * (t + 1)), a_codes[:], a_scales[:])
+            filters[n] = bank[:].rearrange("p (d v) -> p d v", d=D)
+            if t >= PLAIN[c]:
+                copied = ring.tile([P, D, LOAD], F32, name="filter", bufs=4)
+                nc.scalar.copy(out=copied[:], in_=filters[n])
+                filters[n] = copied
 
         def multiply(n):
-            v0, width, t = steps[n]
-            blocks = width // P
-            half, in_half = divmod(v0, HALF)
-            pair, tt = divmod(t, 2)
-            picked = early_view(tt, half)[:, :, in_half : in_half + width]
-            terms = ring.tile([P, D, width], F32, name="terms", bufs=4)
-            nc.vector.tensor_tensor(
-                out=terms[:], in0=filters[n], in1=picked, op=MULT
-            )
-            if pair == 0:
-                gather(t + 2, v0, width, picked)
+            c, t = steps[n]
             if t == 0:
-                z_rows[v0] = ring.tile([P, blocks * H], BF16, name="z_rows")
-            if tt == 0:
-                z_sums[v0, pair] = psum.tile([P, blocks, 2 * P], F32, name="z_sum", bufs=2)
-            z_sum = z_sums[v0, pair]
-            for b in range(blocks):
+                terms[c] = ring.tile([P, D, TILES, LOAD], F32, name="terms", bufs=2)
+            if t >= PLAIN[c]:
                 for d in range(D):
-                    nc.tensor.matmul(
-                        z_sum[:, b, P * tt : P * (tt + 1)],
-                        lhsT=terms[:, d, P * b : P * (b + 1)],
-                        rhs=identity[:],
-                        is_transpose=True,
-                        start=(d == 0),
-                        stop=(d == D - 1),
+                    offsets = lists[d][:, LOAD // 16 * c : LOAD // 16 * (c + 1)]
+                    nc.vector.tensor_tensor(
+                        out=terms[c][:, d, t, :], in0=h[t][:].indirect(offsets), in1=filters[n][:, d, :], op=MULT
                     )
-            if tt == 1:
-                z_view = z_rows[v0][:].rearrange("v (b u p e) -> v b u p e", b=blocks, u=2, e=2)
-                nc.scalar.copy(
-                    out=z_view[:, :, :, 64 * pair : 64 * (pair + 1), :],
-                    in_=z_sum[:].rearrange("v b (p u e) -> v b u p e", u=2, e=2),
+            else:
+                half, in_half = divmod(LOAD * c, HALF)
+                picked = early[t, half][:].rearrange("p (d v) -> p d v", d=D)[:, :, in_half : in_half + LOAD]
+                nc.vector.tensor_tensor(out=terms[c][:, :, t, :], in0=filters[n], in1=picked, op=MULT)
+
+        def project(c):
+            pieces = 2 if c == CHUNKS - 1 else 1
+            width = LOAD // pieces
+            staged = []
+            for piece in range(pieces):
+                z_staged = ring.tile([P, PACK * width], BF16, name="z_staged", align_bytes=64)
+                first, second = [
+                    terms[c][:, d, :, width * piece : width * (piece + 1)].rearrange("p j (c i) -> p c j i", i=RUN)
+                    for d in range(D)
+                ]
+                nc.vector.tensor_tensor(
+                    out=z_staged[:].rearrange("p (c i j) -> p c j i", i=RUN, j=PACK), in0=first, in1=second, op=ADD
                 )
+                staged.append(z_staged)
+            for piece in range(pieces):
+                v0 = LOAD * c + width * piece
+                z_codes, z_scales = quantize("z%d" % v0, staged[piece][:])
+                result = psum.tile([P, width], F32, name="result", bufs=2)
+                product(result[:], w2_q, slice(0, N), z_codes[:], z_scales[:])
+                stored = ring.tile([P, width], F32, name="stored")
+                nc.scalar.copy(out=stored[:], in_=result[:])
+                nc.sync.dma_start(out=out[:, v0 : v0 + width], in_=stored[:])
 
-        def project(v0, width):
-            blocks = width // P
-            words = z_rows[v0][:].bitcast(F32)
-            back = psum.tile([P, blocks, 2, P], F32, name="back", bufs=1)
-            for b in range(blocks):
-                for u in range(2):
-                    nc.tensor.transpose(back[:, b, u, :], words[:, P * (2 * b + u) : P * (2 * b + u + 1)], identity[:])
-            z_staged = ring.tile([P, PACK * width], BF16, name="z_staged", align_bytes=64)
-            nc.scalar.copy(
-                out=z_staged[:].bitcast(F32).rearrange("p (b v u) -> p b v u", b=blocks, u=2),
-                in_=back[:].rearrange("p b u v -> p b v u"),
-            )
-            z_codes, z_scales = quantize("z%d" % v0, z_staged[:])
-            result = psum.tile([P, width], F32, name="result")
-            product(result[:], w2_q, slice(0, N), z_codes[:], z_scales[:])
-            stored = ring.tile([P, width], F32, name="stored")
-            nc.scalar.copy(out=stored[:], in_=result[:])
-            nc.sync.dma_start(out=out[:, v0 : v0 + width], in_=stored[:])
-
-        LEAD, TAIL = 2, 1
+        LEAD = 2
         for n in range(LEAD):
             filter_product(n)
-        for n in range(len(steps) + TAIL):
+        for n in range(len(steps)):
             if n == 0:
                 a_q.append(quantize_a(1, a_ring()))
             if n == 2:
@@ -250,7 +240,6 @@ def tile_picked_wdime_none_l_kernel(
                 a_q.append(quantize_a(3, a_ring()))
             if n + LEAD < len(steps):
                 filter_product(n + LEAD)
-            if n < len(steps):
-                multiply(n)
-            if n >= TAIL and steps[n - TAIL][2] == TILES - 1:
-                project(*steps[n - TAIL][:2])
+            multiply(n)
+            if steps[n][1] == TILES - 1:
+                project(steps[n][0])

@@ -19,27 +19,24 @@ ADD = mybir.AluOpType.add
 P = 128
 PACK = 4
 BANK = 512
+GROUP = 16
+BLOCKS = H // 32
+LANES = 8
 TILES = H // P
 PASSES = K // (P * PACK)
 HALF = T // 2
-LOAD = 256
-CHUNKS = T // LOAD
-X_PIECES = ((0, 512), (512, 512))
-PLAIN = (2, 2, 2, 2)
+CHUNK = BANK // D
+CHUNKS = T // CHUNK
 RUN = 2
+EARLY = (T, HALF)
+LEAD = 2
+LAST_PIECES = 2
 
 
 def interleave(copy, staged, raw):
     copy(
         out=staged.rearrange("p (c i j) -> p c j i", i=RUN, j=PACK),
         in_=raw.rearrange("p j (c i) -> p c j i", i=RUN),
-    )
-
-
-def deal(copy, staged, raw, t):
-    copy(
-        out=staged.rearrange("p (b r i j) -> p b r j i", b=16, i=RUN, j=PACK),
-        in_=raw.rearrange("p j (b t r i) -> p t b r j i", b=16, t=TILES, i=RUN)[:, t],
     )
 
 
@@ -55,6 +52,9 @@ def tile_picked_wdime_none_l_kernel(
         def held(name, width, dtype):
             return keep.tile([P, width], dtype, name=name, align_bytes=64)
 
+        def accumulator():
+            return psum.tile([P, BANK], F32, name="acc", bufs=6)
+
         def quantize(name, staged):
             words = staged.shape[1] // PACK
             codes = held(name + "_codes", words, U32)
@@ -62,13 +62,14 @@ def tile_picked_wdime_none_l_kernel(
             nc.vector.quantize_mx(out=codes[:].bitcast(FP8X4), scales=scales[:], in_=staged)
             return codes, scales
 
-        def product(acc, lhs, lhs_cols, rhs_codes, rhs_scales, start=True, stop=True):
+        def product(acc, weights, columns, moving_codes, moving_scales, start=True, stop=True):
+            codes, scales = weights
             nc.tensor.matmul_mx(
                 out=acc,
-                lhsT=lhs[0][:, lhs_cols].bitcast(FP8X4),
-                lhsT_scale=lhs[1][:, lhs_cols],
-                rhs=rhs_codes.bitcast(FP8X4),
-                rhs_scale=rhs_scales,
+                lhsT=codes[:, columns].bitcast(FP8X4),
+                lhsT_scale=scales[:, columns],
+                rhs=moving_codes.bitcast(FP8X4),
+                rhs_scale=moving_scales,
                 start=start,
                 stop=stop,
             )
@@ -77,169 +78,188 @@ def tile_picked_wdime_none_l_kernel(
         nc.vector.memset(x_planes[:].bitcast(U32), 0)
 
         w1_raw = []
-        for z in range(PASSES):
-            raw = keep.tile([P, PACK, H], F32, name="w1_raw%d" % z)
-            nc.sync.dma_start(out=raw[:], in_=w1.rearrange("(z p j) c -> z p j c", z=PASSES, j=PACK)[z])
+        for g in range(PASSES):
+            raw = keep.tile([P, PACK, H], F32, name="w1_raw%d" % g)
+            nc.sync.dma_start(out=raw[:], in_=w1.rearrange("(g p j) c -> g p j c", g=PASSES, j=PACK)[g])
             w1_raw.append(raw)
-        for q in range(4):
+        for q in range(P // 32):
             nc.sync.dma_start(
                 out=x_planes[32 * q : 32 * q + 4 * PASSES, :].bitcast(I32),
                 in_=x_scales[:, 4 * q : 4 * q + 4, :].bitcast(I32),
             )
-        x_rows = x_words.rearrange("z p c r -> p z (c r)")
+        x_rows = x_words.rearrange("g p c j -> p g (c j)")
         x_codes = []
-        for c0, width in X_PIECES:
-            codes = keep.tile([P, PASSES, width], U32, name="x_codes%d" % c0, align_bytes=64)
+        for c0 in range(0, T, HALF):
+            codes = keep.tile([P, PASSES, HALF], U32, name="x_codes%d" % c0, align_bytes=64)
             nc.sync.dma_start(
                 out=codes[:].bitcast(I32),
-                in_=x_rows[:, :, PACK * c0 : PACK * (c0 + width)].bitcast(I32),
+                in_=x_rows[:, :, PACK * c0 : PACK * (c0 + HALF)].bitcast(I32),
             )
             x_codes.append(codes)
         lists = []
         for d, pos in enumerate((pos1, pos2)):
-            offsets = keep.tile([P, T // 16], U16, name="pos%d" % d)
+            offsets = keep.tile([P, T // GROUP], U16, name="pos%d" % d)
             nc.sync.dma_start(offsets[:], pos)
             lists.append(offsets)
         w3_raw = keep.tile([P, PACK, H], F32, name="w3_raw")
         nc.sync.dma_start(out=w3_raw[:], in_=w3.rearrange("(p j) c -> p j c", j=PACK))
         a_rows = aT.rearrange("(p j) (d v) -> p (j d) v", j=PACK, d=D)
         a_raw = []
-        w2_raw = keep.tile([P, PACK, N], F32, name="w2_raw")
-        for c in range(T // LOAD):
-            raw = keep.tile([P, PACK * D, LOAD], F32, name="a_raw%d" % c)
-            nc.sync.dma_start(out=raw[:], in_=a_rows[:, :, LOAD * c : LOAD * (c + 1)])
+        w2_raw = keep.tile([P, TILES, N], F32, name="w2_raw")
+        for c in range(CHUNKS):
+            raw = keep.tile([P, PACK * D, CHUNK], F32, name="a_raw%d" % c)
+            nc.sync.dma_start(out=raw[:], in_=a_rows[:, :, CHUNK * c : CHUNK * (c + 1)])
             a_raw.append(raw)
             if c == 1:
                 for t in range(TILES):
-                    nc.sync.dma_start(out=w2_raw[:, t, :], in_=w2.rearrange("(b t r) m -> t b r m", t=TILES, r=8)[t])
+                    nc.sync.dma_start(
+                        out=w2_raw[:, t, :], in_=w2.rearrange("(b t r) m -> t b r m", t=TILES, r=LANES)[t]
+                    )
+
+        def deal_w1(staged, g, t):
+            nc.vector.tensor_copy(
+                out=staged.rearrange("p (b r i j) -> p b r j i", b=BLOCKS, i=RUN, j=PACK),
+                in_=w1_raw[g][:].rearrange("p j (b t r i) -> p t b r j i", b=BLOCKS, t=TILES, i=RUN)[:, t],
+            )
 
         w1_q = {}
-        for z in range(PASSES):
-            staged = [held("w1_staged%d%d" % (z, t), BANK, BF16)[:] for t in range(TILES)]
-            deal(nc.vector.tensor_copy, staged[0], w1_raw[z][:], 0)
+        for g in range(PASSES):
+            staged = [held("w1_staged%d%d" % (g, t), PACK * P, BF16)[:] for t in range(TILES)]
+            deal_w1(staged[0], g, 0)
             for t in range(TILES):
                 if t + 1 < TILES:
-                    deal(nc.vector.tensor_copy, staged[t + 1], w1_raw[z][:], t + 1)
-                w1_q[z, t] = quantize("w1_%d%d" % (z, t), staged[t])
+                    deal_w1(staged[t + 1], g, t + 1)
+                w1_q[g, t] = quantize("w1_%d%d" % (g, t), staged[t])
 
         h = []
 
         def h_tile(t):
             h_t = keep.tile([P, T], F32, name="h%d" % t)
-            for codes, (c0, width) in zip(x_codes, X_PIECES):
-                acc = psum.tile([P, width], F32, name="acc", bufs=6)
-                for z in range(PASSES):
+            width = BANK // 2 if t == 0 else BANK
+            for c0 in range(0, T, width):
+                half, first = divmod(c0, HALF)
+                acc = accumulator()[:, :width]
+                for g in range(PASSES):
                     product(
-                        acc[:], w1_q[z, t], slice(0, P),
-                        codes[:, z, :], x_planes[4 * z :, c0 : c0 + width],
-                        start=(z == 0), stop=(z == PASSES - 1),
+                        acc, w1_q[g, t], slice(0, P),
+                        x_codes[half][:, g, first : first + width], x_planes[4 * g :, c0 : c0 + width],
+                        start=(g == 0), stop=(g == PASSES - 1),
                     )
-                nc.scalar.activation(out=h_t[:, c0 : c0 + width], in_=acc[:], func=SILU)
+                nc.scalar.activation(out=h_t[:, c0 : c0 + width], in_=acc, func=SILU)
             h.append(h_t)
 
-        early = {}
+        def looked_up(t, d, v0, width):
+            return h[t][:].indirect(lists[d][:, v0 // GROUP : (v0 + width) // GROUP])
 
-        def early_tile(t, half):
-            early[t, half] = held("early%d%d" % (t, half), D * HALF, F32)
-            return early[t, half]
+        early = [held("early%d" % t, D * T, F32) for t in range(len(EARLY))]
 
-        def gather_early(t, half):
-            for d in range(D):
-                offsets = lists[d][:, HALF // 16 * half : HALF // 16 * (half + 1)]
-                nc.vector.tensor_copy(out=early[t, half][:, HALF * d : HALF * (d + 1)], in_=h[t][:].indirect(offsets))
+        def gather_early(t, d, v0):
+            nc.vector.tensor_copy(out=early[t][:, T * d + v0 : T * d + v0 + HALF], in_=looked_up(t, d, v0, HALF))
+
+        def is_early(c, t):
+            return t < len(EARLY) and CHUNK * c < EARLY[t]
 
         def quantize_a(c, staged):
-            interleave(nc.scalar.copy, staged, a_raw[c][:].rearrange("p (j d) v -> p j (d v)", j=PACK))
+            raw = a_raw[c][:].rearrange("p (j d) v -> p j (d v)", j=PACK)
+            for d in range(D):
+                interleave(
+                    nc.scalar.copy,
+                    staged[:, PACK * CHUNK * d : PACK * CHUNK * (d + 1)],
+                    raw[:, :, CHUNK * d : CHUNK * (d + 1)],
+                )
             return quantize("a%d" % c, staged)
 
-        def a_ring():
-            return ring.tile([P, PACK * D * LOAD], BF16, name="a_staged", align_bytes=64)[:]
-
-        units = [(t, half) for t in range(TILES) for half in range(2) if t < PLAIN[2 * half]]
-        for unit in units:
-            early_tile(*unit)
         h_tile(0)
         h_tile(1)
-        for unit in units[:-2]:
-            gather_early(*unit)
-        staged = early[units[-2]][:].bitcast(BF16)
+        for v0 in range(0, EARLY[0], HALF):
+            for d in range(D):
+                gather_early(0, d, v0)
+
+        staged = held("w3_staged", PACK * H, BF16)[:]
         for t in range(TILES):
-            deal(nc.scalar.copy, staged[:, BANK * t : BANK * (t + 1)], w3_raw[:], t)
+            nc.gpsimd.tensor_scalar(
+                out=staged[:, PACK * P * t : PACK * P * (t + 1)].rearrange("p (b r j) -> p b r j", b=BLOCKS, j=PACK),
+                in0=w3_raw[:].rearrange("p j (b t r) -> p t b r j", b=BLOCKS, t=TILES)[:, t],
+                scalar1=1.0, scalar2=0.0, op0=MULT, op1=ADD,
+            )
         w3_q = quantize("w3", staged)
-        gather_early(*units[-2])
-        a_q = [quantize_a(0, early[units[-1]][:].bitcast(BF16))]
-        gather_early(*units[-1])
+
+        gather_early(1, 0, 0)
+        a_q = [quantize_a(0, early[1][:, T:].bitcast(BF16))]
+        gather_early(1, 1, 0)
         h_tile(2)
         h_tile(3)
 
         steps = [(c, t) for c in range(CHUNKS) for t in range(TILES)]
-        filters, terms = {}, {}
+        filters, terms, a_staged = {}, {}, {}
 
         def filter_product(n):
             c, t = steps[n]
             a_codes, a_scales = a_q[c]
-            bank = psum.tile([P, BANK], F32, name="acc", bufs=6)
+            bank = accumulator()
             product(bank[:], w3_q, slice(P * t, P * (t + 1)), a_codes[:], a_scales[:])
             filters[n] = bank[:].rearrange("p (d v) -> p d v", d=D)
-            if t >= PLAIN[c]:
-                copied = ring.tile([P, D, LOAD], F32, name="filter", bufs=4)
+            if not is_early(c, t):
+                copied = ring.tile([P, D, CHUNK], F32, name="filter", bufs=4)
                 nc.scalar.copy(out=copied[:], in_=filters[n])
                 filters[n] = copied
 
         def multiply(n):
             c, t = steps[n]
             if t == 0:
-                terms[c] = ring.tile([P, D, TILES, LOAD], F32, name="terms", bufs=2)
-            if t >= PLAIN[c]:
-                for d in range(D):
-                    offsets = lists[d][:, LOAD // 16 * c : LOAD // 16 * (c + 1)]
-                    nc.vector.tensor_tensor(
-                        out=terms[c][:, d, t, :], in0=h[t][:].indirect(offsets), in1=filters[n][:, d, :], op=MULT
-                    )
-            else:
-                half, in_half = divmod(LOAD * c, HALF)
-                picked = early[t, half][:].rearrange("p (d v) -> p d v", d=D)[:, :, in_half : in_half + LOAD]
+                terms[c] = ring.tile([P, D, TILES, CHUNK], F32, name="terms")
+            if is_early(c, t):
+                picked = early[t][:].rearrange("p (d v) -> p d v", d=D)[:, :, CHUNK * c : CHUNK * (c + 1)]
                 nc.vector.tensor_tensor(out=terms[c][:, :, t, :], in0=filters[n], in1=picked, op=MULT)
+            else:
+                for d in range(D):
+                    nc.vector.tensor_tensor(
+                        out=terms[c][:, d, t, :],
+                        in0=looked_up(t, d, CHUNK * c, CHUNK),
+                        in1=filters[n][:, d, :],
+                        op=MULT,
+                    )
 
         def project(c):
-            pieces = 2 if c == CHUNKS - 1 else 1
-            width = LOAD // pieces
-            staged = []
-            for piece in range(pieces):
-                z_staged = ring.tile([P, PACK * width], BF16, name="z_staged", align_bytes=64)
+            is_last = c == CHUNKS - 1
+            width = CHUNK // LAST_PIECES if is_last else CHUNK
+            sums = []
+            for v0 in range(0, CHUNK, width):
+                if is_last:
+                    z_staged = ring.tile([P, PACK * width], BF16, name="z_staged", align_bytes=64)[:]
+                else:
+                    z_staged = a_staged[c + 1][:, : PACK * width]
                 first, second = [
-                    terms[c][:, d, :, width * piece : width * (piece + 1)].rearrange("p j (c i) -> p c j i", i=RUN)
-                    for d in range(D)
+                    terms[c][:, d, :, v0 : v0 + width].rearrange("p t (v i) -> p v t i", i=RUN) for d in range(D)
                 ]
                 nc.vector.tensor_tensor(
-                    out=z_staged[:].rearrange("p (c i j) -> p c j i", i=RUN, j=PACK), in0=first, in1=second, op=ADD
+                    out=z_staged.rearrange("p (v i t) -> p v t i", i=RUN, t=TILES), in0=first, in1=second, op=ADD
                 )
-                staged.append(z_staged)
-            for piece in range(pieces):
-                v0 = LOAD * c + width * piece
-                z_codes, z_scales = quantize("z%d" % v0, staged[piece][:])
+                sums.append((CHUNK * c + v0, z_staged))
+            for target, z_staged in sums:
+                z_codes, z_scales = quantize("z%d" % target, z_staged)
                 result = psum.tile([P, width], F32, name="result", bufs=2)
                 product(result[:], w2_q, slice(0, N), z_codes[:], z_scales[:])
                 stored = ring.tile([P, width], F32, name="stored")
                 nc.scalar.copy(out=stored[:], in_=result[:])
-                nc.sync.dma_start(out=out[:, v0 : v0 + width], in_=stored[:])
+                nc.sync.dma_start(out=out[:, target : target + width], in_=stored[:])
 
-        LEAD = 2
         for n in range(LEAD):
             filter_product(n)
         for n in range(len(steps)):
-            if n == 0:
-                a_q.append(quantize_a(1, a_ring()))
-            if n == 2:
+            c, t = steps[n]
+            ahead = n + LEAD
+            if ahead < len(steps) and steps[ahead][1] == 0:
+                a_staged[c + 1] = ring.tile(
+                    [P, PACK * D * CHUNK], BF16, name="a_staged", align_bytes=64, bufs=CHUNKS - 1
+                )[:]
+                a_q.append(quantize_a(c + 1, a_staged[c + 1]))
+            if n == TILES - 1:
                 staged = held("w2_staged", PACK * N, BF16)[:]
                 interleave(nc.scalar.copy, staged, w2_raw[:])
                 w2_q = quantize("w2", staged)
-            if n == 4:
-                a_q.append(quantize_a(2, a_ring()))
-            if n == 8:
-                a_q.append(quantize_a(3, a_ring()))
-            if n + LEAD < len(steps):
-                filter_product(n + LEAD)
+            if ahead < len(steps):
+                filter_product(ahead)
             multiply(n)
-            if steps[n][1] == TILES - 1:
-                project(steps[n][0])
+            if t == TILES - 1:
+                project(c)

from contextlib import ExitStack

import concourse.mybir as mybir

K, T, H, N, J, D = 1024, 1024, 512, 128, 512, 2
FLOPS = 2 * (K * H * T + J * H * D * T + H * N * T)

F32 = mybir.dt.float32
BF16 = mybir.dt.bfloat16
I32 = mybir.dt.int32
U32 = mybir.dt.uint32
U16 = mybir.dt.uint16
U8 = mybir.dt.uint8
FP8X4 = mybir.dt.float8_e4m3fn_x4
SILU = mybir.ActivationFunctionType.Silu
MULT = mybir.AluOpType.mult
ADD = mybir.AluOpType.add

P = 128
PACK = 4
BANK = 512
GROUP = 16
BLOCKS = H // 32
LANES = 8
TILES = H // P
PASSES = K // (P * PACK)
HALF = T // 2
CHUNK = BANK // D
CHUNKS = T // CHUNK
RUN = 2
EARLY = (T, HALF)
LEAD = 2
LAST_PIECES = 2


def interleave(copy, staged, raw):
    copy(
        out=staged.rearrange("p (c i j) -> p c j i", i=RUN, j=PACK),
        in_=raw.rearrange("p j (c i) -> p c j i", i=RUN),
    )


def tile_picked_wdime_none_l_kernel(
    tc, x_words, x_scales, aT, w1, w3, w2, pos1, pos2, out
):
    nc = tc.nc
    with ExitStack() as ctx:
        keep = ctx.enter_context(tc.tile_pool(name="keep", bufs=1))
        ring = ctx.enter_context(tc.tile_pool(name="ring", bufs=2))
        psum = ctx.enter_context(tc.psum_pool(name="psum", bufs=1))

        def held(name, width, dtype):
            return keep.tile([P, width], dtype, name=name, align_bytes=64)

        def accumulator():
            return psum.tile([P, BANK], F32, name="acc", bufs=6)

        def quantize(name, staged):
            words = staged.shape[1] // PACK
            codes = held(name + "_codes", words, U32)
            scales = held(name + "_scales", words, U8)
            nc.vector.quantize_mx(out=codes[:].bitcast(FP8X4), scales=scales[:], in_=staged)
            return codes, scales

        def product(acc, weights, columns, moving_codes, moving_scales, start=True, stop=True):
            codes, scales = weights
            nc.tensor.matmul_mx(
                out=acc,
                lhsT=codes[:, columns].bitcast(FP8X4),
                lhsT_scale=scales[:, columns],
                rhs=moving_codes.bitcast(FP8X4),
                rhs_scale=moving_scales,
                start=start,
                stop=stop,
            )

        x_planes = held("x_planes", T, U8)
        nc.vector.memset(x_planes[:].bitcast(U32), 0)

        w1_raw = []
        for g in range(PASSES):
            raw = keep.tile([P, PACK, H], F32, name="w1_raw%d" % g)
            nc.sync.dma_start(out=raw[:], in_=w1.rearrange("(g p j) c -> g p j c", g=PASSES, j=PACK)[g])
            w1_raw.append(raw)
        for q in range(P // 32):
            nc.sync.dma_start(
                out=x_planes[32 * q : 32 * q + 4 * PASSES, :].bitcast(I32),
                in_=x_scales[:, 4 * q : 4 * q + 4, :].bitcast(I32),
            )
        x_rows = x_words.rearrange("g p c j -> p g (c j)")
        x_codes = []
        for c0 in range(0, T, HALF):
            codes = keep.tile([P, PASSES, HALF], U32, name="x_codes%d" % c0, align_bytes=64)
            nc.sync.dma_start(
                out=codes[:].bitcast(I32),
                in_=x_rows[:, :, PACK * c0 : PACK * (c0 + HALF)].bitcast(I32),
            )
            x_codes.append(codes)
        lists = []
        for d, pos in enumerate((pos1, pos2)):
            offsets = keep.tile([P, T // GROUP], U16, name="pos%d" % d)
            nc.sync.dma_start(offsets[:], pos)
            lists.append(offsets)
        w3_raw = keep.tile([P, PACK, H], F32, name="w3_raw")
        nc.sync.dma_start(out=w3_raw[:], in_=w3.rearrange("(p j) c -> p j c", j=PACK))
        a_rows = aT.rearrange("(p j) (d v) -> p (j d) v", j=PACK, d=D)
        a_raw = []
        w2_raw = keep.tile([P, TILES, N], F32, name="w2_raw")
        for c in range(CHUNKS):
            raw = keep.tile([P, PACK * D, CHUNK], F32, name="a_raw%d" % c)
            nc.sync.dma_start(out=raw[:], in_=a_rows[:, :, CHUNK * c : CHUNK * (c + 1)])
            a_raw.append(raw)
            if c == 1:
                for t in range(TILES):
                    nc.sync.dma_start(
                        out=w2_raw[:, t, :], in_=w2.rearrange("(b t r) m -> t b r m", t=TILES, r=LANES)[t]
                    )

        def deal_w1(staged, g, t):
            nc.vector.tensor_copy(
                out=staged.rearrange("p (b r i j) -> p b r j i", b=BLOCKS, i=RUN, j=PACK),
                in_=w1_raw[g][:].rearrange("p j (b t r i) -> p t b r j i", b=BLOCKS, t=TILES, i=RUN)[:, t],
            )

        w1_q = {}
        for g in range(PASSES):
            staged = [held("w1_staged%d%d" % (g, t), PACK * P, BF16)[:] for t in range(TILES)]
            deal_w1(staged[0], g, 0)
            for t in range(TILES):
                if t + 1 < TILES:
                    deal_w1(staged[t + 1], g, t + 1)
                w1_q[g, t] = quantize("w1_%d%d" % (g, t), staged[t])

        h = []

        def h_tile(t):
            h_t = keep.tile([P, T], F32, name="h%d" % t)
            width = BANK // 2 if t == 0 else BANK
            for c0 in range(0, T, width):
                half, first = divmod(c0, HALF)
                acc = accumulator()[:, :width]
                for g in range(PASSES):
                    product(
                        acc, w1_q[g, t], slice(0, P),
                        x_codes[half][:, g, first : first + width], x_planes[4 * g :, c0 : c0 + width],
                        start=(g == 0), stop=(g == PASSES - 1),
                    )
                nc.scalar.activation(out=h_t[:, c0 : c0 + width], in_=acc, func=SILU)
            h.append(h_t)

        def looked_up(t, d, v0, width):
            return h[t][:].indirect(lists[d][:, v0 // GROUP : (v0 + width) // GROUP])

        early = [held("early%d" % t, D * T, F32) for t in range(len(EARLY))]

        def gather_early(t, d, v0):
            nc.vector.tensor_copy(out=early[t][:, T * d + v0 : T * d + v0 + HALF], in_=looked_up(t, d, v0, HALF))

        def is_early(c, t):
            return t < len(EARLY) and CHUNK * c < EARLY[t]

        def quantize_a(c, staged):
            raw = a_raw[c][:].rearrange("p (j d) v -> p j (d v)", j=PACK)
            for d in range(D):
                interleave(
                    nc.scalar.copy,
                    staged[:, PACK * CHUNK * d : PACK * CHUNK * (d + 1)],
                    raw[:, :, CHUNK * d : CHUNK * (d + 1)],
                )
            return quantize("a%d" % c, staged)

        h_tile(0)
        h_tile(1)
        for v0 in range(0, EARLY[0], HALF):
            for d in range(D):
                gather_early(0, d, v0)

        staged = held("w3_staged", PACK * H, BF16)[:]
        for t in range(TILES):
            nc.gpsimd.tensor_scalar(
                out=staged[:, PACK * P * t : PACK * P * (t + 1)].rearrange("p (b r j) -> p b r j", b=BLOCKS, j=PACK),
                in0=w3_raw[:].rearrange("p j (b t r) -> p t b r j", b=BLOCKS, t=TILES)[:, t],
                scalar1=1.0, scalar2=0.0, op0=MULT, op1=ADD,
            )
        w3_q = quantize("w3", staged)

        gather_early(1, 0, 0)
        a_q = [quantize_a(0, early[1][:, T:].bitcast(BF16))]
        gather_early(1, 1, 0)
        h_tile(2)
        h_tile(3)

        steps = [(c, t) for c in range(CHUNKS) for t in range(TILES)]
        filters, terms, a_staged = {}, {}, {}

        def filter_product(n):
            c, t = steps[n]
            a_codes, a_scales = a_q[c]
            bank = accumulator()
            product(bank[:], w3_q, slice(P * t, P * (t + 1)), a_codes[:], a_scales[:])
            filters[n] = bank[:].rearrange("p (d v) -> p d v", d=D)
            if not is_early(c, t):
                copied = ring.tile([P, D, CHUNK], F32, name="filter", bufs=4)
                nc.scalar.copy(out=copied[:], in_=filters[n])
                filters[n] = copied

        def multiply(n):
            c, t = steps[n]
            if t == 0:
                terms[c] = ring.tile([P, D, TILES, CHUNK], F32, name="terms")
            if is_early(c, t):
                picked = early[t][:].rearrange("p (d v) -> p d v", d=D)[:, :, CHUNK * c : CHUNK * (c + 1)]
                nc.vector.tensor_tensor(out=terms[c][:, :, t, :], in0=filters[n], in1=picked, op=MULT)
            else:
                for d in range(D):
                    nc.vector.tensor_tensor(
                        out=terms[c][:, d, t, :],
                        in0=looked_up(t, d, CHUNK * c, CHUNK),
                        in1=filters[n][:, d, :],
                        op=MULT,
                    )

        def project(c):
            is_last = c == CHUNKS - 1
            width = CHUNK // LAST_PIECES if is_last else CHUNK
            sums = []
            for v0 in range(0, CHUNK, width):
                if is_last:
                    z_staged = ring.tile([P, PACK * width], BF16, name="z_staged", align_bytes=64)[:]
                else:
                    z_staged = a_staged[c + 1][:, : PACK * width]
                first, second = [
                    terms[c][:, d, :, v0 : v0 + width].rearrange("p t (v i) -> p v t i", i=RUN) for d in range(D)
                ]
                nc.vector.tensor_tensor(
                    out=z_staged.rearrange("p (v i t) -> p v t i", i=RUN, t=TILES), in0=first, in1=second, op=ADD
                )
                sums.append((CHUNK * c + v0, z_staged))
            for target, z_staged in sums:
                z_codes, z_scales = quantize("z%d" % target, z_staged)
                result = psum.tile([P, width], F32, name="result", bufs=2)
                product(result[:], w2_q, slice(0, N), z_codes[:], z_scales[:])
                stored = ring.tile([P, width], F32, name="stored")
                nc.scalar.copy(out=stored[:], in_=result[:])
                nc.sync.dma_start(out=out[:, target : target + width], in_=stored[:])

        for n in range(LEAD):
            filter_product(n)
        for n in range(len(steps)):
            c, t = steps[n]
            ahead = n + LEAD
            if ahead < len(steps) and steps[ahead][1] == 0:
                a_staged[c + 1] = ring.tile(
                    [P, PACK * D * CHUNK], BF16, name="a_staged", align_bytes=64, bufs=CHUNKS - 1
                )[:]
                a_q.append(quantize_a(c + 1, a_staged[c + 1]))
            if n == TILES - 1:
                staged = held("w2_staged", PACK * N, BF16)[:]
                interleave(nc.scalar.copy, staged, w2_raw[:])
                w2_q = quantize("w2", staged)
            if ahead < len(steps):
                filter_product(ahead)
            multiply(n)
            if t == TILES - 1:
                project(c)
